import numpy as np
import ml_dtypes


def mxq(x, axis, fmt="e4m3"):
    dtype, down = {"e4m3": (ml_dtypes.float8_e4m3fn, 7), "e5m2": (ml_dtypes.float8_e5m2, 14)}[fmt]
    v = np.moveaxis(np.asarray(x, np.float32).astype(ml_dtypes.bfloat16).astype(np.float64), axis, -1)
    blocks = v.reshape(v.shape[:-1] + (-1, 32))
    amax = np.abs(blocks).max(-1, keepdims=True)
    byte = np.maximum(np.where(amax > 0, np.frexp(amax)[1] - 1 + 127, 0) - down, 1)
    scale = np.exp2(byte - 127.0)
    codes = (blocks / scale).astype(np.float32).astype(dtype).astype(np.float64)
    return np.moveaxis((codes * scale).reshape(v.shape), -1, axis)


WIDE = False


def mx_kscale(k):
    if not WIDE:
        return np.ones(k)
    levels = np.array([10, -10, 5, -5, 0])
    if k % 512:
        return np.exp2(np.random.permutation(np.resize(levels, k // 32))).repeat(32)
    a = np.empty((k // 512, 16))
    for p in range(k // 512):
        a[p, :8] = np.random.permutation(np.resize(levels, 8))
        for g in range(8):
            far = levels[np.abs(levels - a[p, g]) >= 10]
            a[p, g + 8] = far[np.random.randint(len(far))]
    return np.exp2(a.ravel()).repeat(32)


def f64(x):
    return np.asarray(x).astype(np.float64)


def striped(idx):
    return np.tile(idx.reshape(-1, 16).T, (8, 1)).astype(np.uint16)


def unstriped(offs):
    return offs[:16].T.reshape(-1).astype(np.int64)


E2M1 = np.array([0.0, 0.5, 1.0, 1.5, 2.0, 3.0, 4.0, 6.0, -0.0, -0.5, -1.0, -1.5, -2.0, -3.0, -4.0, -6.0])


def pack_weight(w, fmt):
    k, n = w.shape
    w = f64(np.asarray(w, np.float32).astype(ml_dtypes.bfloat16)).reshape(k // 32, 32, n)
    amax = np.abs(w).max(1)
    if fmt == "e4m3":
        byte = np.frexp(amax)[1] - 1 + 127 - 7
    else:
        mant, ex = np.frexp(amax / 6.0)
        byte = np.where(mant > 0.5, ex, ex - 1) + 127
    byte = np.clip(np.where(amax > 0, byte, 1), 1, 254)
    scaled = (w * np.exp2(127.0 - byte)[:, None, :]).reshape(k, n).astype(np.float32)
    by_word = np.ascontiguousarray(scaled.reshape(k // 512, 128, 4, n).transpose(0, 1, 3, 2))
    if fmt == "e4m3":
        words = by_word.astype(ml_dtypes.float8_e4m3fn).view(np.uint8)
    else:
        c = by_word.astype(ml_dtypes.float4_e2m1fn).view(np.uint8) & 0xF
        words = (c[..., 0::2] | (c[..., 1::2] << 4)).reshape(k // 512, 128, 2 * n)
    return np.ascontiguousarray(words), np.ascontiguousarray(byte.astype(np.uint8).reshape(k // 512, 16, n))


def unpack_weight(words, scales, fmt):
    g, _, n = scales.shape
    words = np.ascontiguousarray(words).reshape(g, 128, n, -1)
    if fmt == "e4m3":
        vals = words.view(ml_dtypes.float8_e4m3fn).astype(np.float64)
    else:
        nib = np.empty((g, 128, n, 4), np.uint8)
        nib[..., 0::2] = words & 0xF
        nib[..., 1::2] = words >> 4
        vals = E2M1[nib]
    vals = vals * np.repeat(np.exp2(scales.astype(np.float64) - 127.0), 8, axis=1)[..., None]
    return vals.transpose(0, 1, 3, 2).reshape(g * 512, n)


def silu(v):
    return v / (1.0 + np.exp(-np.maximum(v, -700.0)))


G, K, M, T, S = 2, 512, 256, 2048, 512


def setup_inputs():
    n = np.random.standard_normal
    s = mx_kscale(K)[:, None]
    p_w4 = pack_weight(n((K, M)) / np.sqrt(K) / s, "e2m1")
    p_w8 = pack_weight(n((K, M)) / np.sqrt(K) / s, "e4m3")
    return {
        "xT": (n((K, T)) * s).astype(np.float32),
        "c": (n((K, S)) * s).astype(np.float32),
        "w4_words": p_w4[0],
        "w4_scales": p_w4[1],
        "w8_words": p_w8[0],
        "w8_scales": p_w8[1],
        "b": (0.3 * n(256)).astype(np.float32),
        "offs": striped(np.concatenate([np.random.permutation(T)[:S] for _ in range(G)])),
    }


def reference(xT, c, w4_words, w4_scales, w8_words, w8_scales, b, offs):
    idx = unstriped(offs).reshape(G, S)
    xm_ = mxq(np.max([f64(xT)[:, idx[g]] for g in range(G)], axis=0), 0, "e4m3")
    c_ = mxq(f64(c), 0, "e4m3")
    w4_ = unpack_weight(w4_words, w4_scales, "e2m1")
    w8_ = unpack_weight(w8_words, w8_scales, "e4m3")
    y = xm_.T @ w4_ + c_.T @ w8_
    return silu(y + f64(b)[None, :])

@@ -1,0 +1,195 @@
+from contextlib import ExitStack
+
+import concourse.mybir as mybir
+from concourse.masks import make_identity
+
+G, K, M, T, S = 2, 512, 256, 2048, 512
+FLOPS = 2 * 2 * K * M * S
+
+F32 = mybir.dt.float32
+BF16 = mybir.dt.bfloat16
+U32 = mybir.dt.uint32
+I32 = mybir.dt.int32
+U16 = mybir.dt.uint16
+U8 = mybir.dt.uint8
+FP8X4 = mybir.dt.float8_e4m3fn_x4
+FP4X4 = mybir.dt.float4_e2m1fn_x4
+ACT = mybir.ActivationFunctionType
+ALU = mybir.AluOpType
+
+P = 128
+PACK = 4
+RUN = 4
+HALF = S // 2
+LANES = 16
+
+X_CHUNKS = ((0, 0, 1024, 0), (0, 1024, 2048, 704), (1, 0, 1024, 0), (1, 1024, 1664, 640), (1, 1664, 2048, 256))
+
+
+def tile_list_sage_tm_silu_kernel(tc, xT, c, w4_words, w4_scales, w8_words, w8_scales, b, offs, out):
+    nc = tc.nc
+    with ExitStack() as ctx:
+        keep = ctx.enter_context(tc.tile_pool(name="keep", bufs=1))
+        psum = ctx.enter_context(tc.psum_pool(name="psum", bufs=1))
+
+        offsets = keep.tile([P, G * S // LANES], U16, name="offsets")
+        x_rows = xT.rearrange("(p i) t -> p i t", i=PACK)
+        c_rows = c.rearrange("(p i) j -> p i j", i=PACK)
+
+        x_raw = [keep.tile([P, 2, t1 - t0], F32, name="x_raw%d" % n) for n, (h, t0, t1, nv) in enumerate(X_CHUNKS)]
+        c_raw = [keep.tile([P, PACK, HALF], F32, name="c_raw%d" % u) for u in range(2)]
+        w4 = keep.tile([P, 2 * M], U8, name="w4", align_bytes=64)
+        w8 = keep.tile([P, 4 * M], U8, name="w8", align_bytes=64)
+        w_scale = keep.tile([P, 2 * M], U8, name="w_scale", align_bytes=64)
+        b_col = keep.tile([P, 2], F32, name="b_col")
+        nc.vector.memset(w_scale[:].bitcast(U32), 0)
+
+        def load_x(n):
+            h, t0, t1, nv = X_CHUNKS[n]
+            nc.sync.dma_start(out=x_raw[n][:], in_=x_rows[:, 2 * h : 2 * h + 2, t0:t1])
+
+        def load_scales(w, src):
+            for q in range(4):
+                nc.sync.dma_start(
+                    out=w_scale[32 * q : 32 * q + 4, w * M : (w + 1) * M].bitcast(I32),
+                    in_=src[0, 4 * q : 4 * q + 4, :].bitcast(I32),
+                )
+
+        load_x(0)
+        load_x(1)
+        nc.sync.dma_start(offsets[:], offs)
+        nc.sync.dma_start(out=b_col[:], in_=b.rearrange("(p e) -> p e", e=2))
+        load_scales(0, w4_scales)
+        load_x(2)
+        load_x(3)
+        load_x(4)
+        load_scales(1, w8_scales)
+        for u in range(2):
+            nc.sync.dma_start(out=c_raw[u][:], in_=c_rows[:, :, u * HALF : (u + 1) * HALF])
+        nc.sync.dma_start(out=w8[:].bitcast(I32), in_=w8_words[0].rearrange("p n i -> p (n i)").bitcast(I32))
+        nc.sync.dma_start(out=w4[:].bitcast(I32), in_=w4_words[0].bitcast(I32))
+
+        ident = keep.tile([P, P], F32, name="ident")
+        make_identity(nc, ident[:])
+
+        zero = keep.tile([P, 1], F32, name="zero")
+        silu_zero = keep.tile([P, 1], F32, name="silu_zero")
+        nc.vector.memset(zero[:], 0.0)
+        nc.scalar.activation(out=silu_zero[:], in_=zero[:], func=ACT.Silu)
+
+        bias_ps = psum.tile([P, 2, P], F32, name="bias_ps")
+        for e in range(2):
+            nc.tensor.transpose(bias_ps[:, e, :], b_col[:, e : e + 1].to_broadcast([P, P]), ident[:])
+        bias = keep.tile([P, M], F32, name="bias")
+        nc.scalar.activation(
+            out=bias[:].rearrange("p (n e) -> p n e", e=2),
+            in_=bias_ps[:].rearrange("p e n -> p n e"),
+            func=ACT.Identity,
+            bias=silu_zero[:],
+        )
+
+        table = [keep.tile([P, T], U32, name="table%d" % h) for h in range(2)]
+        picked = keep.tile([P, 2, G, S], U32, name="picked")
+
+        def cast_x(n):
+            h, t0, t1, nv = X_CHUNKS[n]
+            for a, z, copy in ((0, nv, nc.vector.tensor_copy), (nv, t1 - t0, nc.scalar.copy)):
+                if z > a:
+                    copy(
+                        table[h][:].bitcast(BF16)[:, 2 * (t0 + a) : 2 * (t0 + z)].rearrange("p (r i e) -> p r e i", i=RUN, e=2),
+                        x_raw[n][:, :, a:z].rearrange("p e (r i) -> p r e i", i=RUN),
+                    )
+
+        def gather(h, g, j0, j1):
+            cols = slice((g * S + j0) // LANES, (g * S + j1) // LANES)
+            nc.vector.tensor_copy(picked[:, h, g, j0:j1], table[h][:].indirect(offsets[:, cols]))
+
+        xm = keep.tile([P, S, PACK], BF16, name="xm", align_bytes=64)
+        cb = keep.tile([P, S, PACK], BF16, name="cb", align_bytes=64)
+        xm_codes = keep.tile([P, S], U32, name="xm_codes", align_bytes=64)
+        xm_scale = keep.tile([P, S], U8, name="xm_scale", align_bytes=64)
+        c_codes = keep.tile([P, S], U32, name="c_codes", align_bytes=64)
+        c_scale = keep.tile([P, S], U8, name="c_scale", align_bytes=64)
+        pairs = picked[:].bitcast(BF16).rearrange("p h g (j e) -> p g j h e", e=2)
+
+        def maximum(j0, j1):
+            nc.vector.tensor_tensor(
+                xm[:, j0:j1, :].rearrange("p j (h e) -> p j h e", e=2),
+                pairs[:, 0, j0:j1],
+                pairs[:, 1, j0:j1],
+                ALU.max,
+            )
+
+        def cast_c(u):
+            nc.scalar.copy(
+                cb[:, u * HALF : (u + 1) * HALF, :].rearrange("p (r i) t -> p r t i", i=RUN),
+                c_raw[u][:].rearrange("p t (r i) -> p r t i", i=RUN),
+            )
+
+        def quantize(codes, scale, src, j0, j1):
+            nc.vector.quantize_mx(
+                out=codes[:, j0:j1].bitcast(FP8X4),
+                scales=scale[:, j0:j1],
+                in_=src[:, j0:j1, :].rearrange("p j t -> p (j t)"),
+            )
+
+        y = [psum.tile([P, M], F32, name="y%d" % jt) for jt in range(S // P)]
+
+        def own_pass(jt):
+            js = slice(jt * P, (jt + 1) * P)
+            nc.tensor.matmul_mx(
+                out=y[jt][:],
+                lhsT=c_codes[:, js].bitcast(FP8X4),
+                lhsT_scale=c_scale[:, js],
+                rhs=w8[:].bitcast(FP8X4),
+                rhs_scale=w_scale[:, M : 2 * M],
+                start=True,
+                stop=False,
+            )
+
+        def neighbour_pass(jt, nh):
+            js = slice(jt * P, (jt + 1) * P)
+            nc.tensor.matmul_mx(
+                out=y[jt][:, nh * P : (nh + 1) * P],
+                lhsT=xm_codes[:, js].bitcast(FP8X4),
+                lhsT_scale=xm_scale[:, js],
+                rhs=w4[:, 2 * nh * P : 2 * (nh + 1) * P].bitcast(FP4X4),
+                rhs_scale=w_scale[:, nh * P : (nh + 1) * P],
+                start=False,
+                stop=(nh == 1),
+            )
+
+        def finish(jt):
+            pre = keep.tile([P, M], F32, name="pre%d" % jt)
+            res = keep.tile([P, M], F32, name="res%d" % jt)
+            nc.vector.tensor_tensor(pre[:], y[jt][:], bias[:], ALU.add)
+            nc.scalar.activation(out=res[:], in_=pre[:], func=ACT.Silu)
+            nc.sync.dma_start(out=out[jt * P : (jt + 1) * P, :], in_=res[:])
+
+        cast_x(0)
+        cast_x(1)
+        gather(0, 0, 0, S)
+        gather(0, 1, 0, S)
+        cast_x(2)
+        cast_x(3)
+        cast_x(4)
+        cast_c(0)
+        cast_c(1)
+        gather(1, 0, 0, HALF)
+        gather(1, 1, 0, HALF)
+        gather(1, 0, HALF, S)
+        maximum(0, HALF)
+        gather(1, 1, HALF, S)
+        quantize(c_codes, c_scale, cb, 0, HALF)
+        quantize(xm_codes, xm_scale, xm, 0, HALF)
+        maximum(HALF, S)
+        quantize(c_codes, c_scale, cb, HALF, S)
+        quantize(xm_codes, xm_scale, xm, HALF, S)
+        for u in range(2):
+            for jt in (2 * u, 2 * u + 1):
+                own_pass(jt)
+            for jt in (2 * u, 2 * u + 1):
+                for nh in range(2):
+                    neighbour_pass(jt, nh)
+        for jt in range(S // P):
+            finish(jt)

@@ -23,7 +23,7 @@ RUN = 4
 HALF = S // 2
 LANES = 16
 
-X_CHUNKS = ((0, 0, 1024, 0), (0, 1024, 2048, 704), (1, 0, 1024, 0), (1, 1024, 1664, 640), (1, 1664, 2048, 256))
+X_CHUNKS = ((0, 0, 1024, 0), (0, 1024, 2048, 704), (1, 0, 896, 0), (1, 896, 1664, 512), (1, 1664, 2048, 256))
 
 
 def tile_list_sage_tm_silu_kernel(tc, xT, c, w4_words, w4_scales, w8_words, w8_scales, b, offs, out):
@@ -37,7 +37,7 @@ def tile_list_sage_tm_silu_kernel(tc, xT, c, w4_words, w4_scales, w8_words, w8_s
         c_rows = c.rearrange("(p i) j -> p i j", i=PACK)
 
         x_raw = [keep.tile([P, 2, t1 - t0], F32, name="x_raw%d" % n) for n, (h, t0, t1, nv) in enumerate(X_CHUNKS)]
-        c_raw = [keep.tile([P, PACK, HALF], F32, name="c_raw%d" % u) for u in range(2)]
+        c_raw = [keep.tile([P, PACK, HALF], F32, name="c_raw%d" % u, align_bytes=64) for u in range(2)]
         w4 = keep.tile([P, 2 * M], U8, name="w4", align_bytes=64)
         w8 = keep.tile([P, 4 * M], U8, name="w8", align_bytes=64)
         w_scale = keep.tile([P, 2 * M], U8, name="w_scale", align_bytes=64)
@@ -48,9 +48,9 @@ def tile_list_sage_tm_silu_kernel(tc, xT, c, w4_words, w4_scales, w8_words, w8_s
             h, t0, t1, nv = X_CHUNKS[n]
             nc.sync.dma_start(out=x_raw[n][:], in_=x_rows[:, 2 * h : 2 * h + 2, t0:t1])
 
-        def load_scales(w, src):
+        def load_scales(queue, w, src):
             for q in range(4):
-                nc.sync.dma_start(
+                queue.dma_start(
                     out=w_scale[32 * q : 32 * q + 4, w * M : (w + 1) * M].bitcast(I32),
                     in_=src[0, 4 * q : 4 * q + 4, :].bitcast(I32),
                 )
@@ -59,15 +59,15 @@ def tile_list_sage_tm_silu_kernel(tc, xT, c, w4_words, w4_scales, w8_words, w8_s
         load_x(1)
         nc.sync.dma_start(offsets[:], offs)
         nc.sync.dma_start(out=b_col[:], in_=b.rearrange("(p e) -> p e", e=2))
-        load_scales(0, w4_scales)
+        load_scales(nc.sync, 1, w8_scales)
         load_x(2)
         load_x(3)
         load_x(4)
-        load_scales(1, w8_scales)
         for u in range(2):
             nc.sync.dma_start(out=c_raw[u][:], in_=c_rows[:, :, u * HALF : (u + 1) * HALF])
         nc.sync.dma_start(out=w8[:].bitcast(I32), in_=w8_words[0].rearrange("p n i -> p (n i)").bitcast(I32))
         nc.sync.dma_start(out=w4[:].bitcast(I32), in_=w4_words[0].bitcast(I32))
+        load_scales(nc.sync, 0, w4_scales)
 
         ident = keep.tile([P, P], F32, name="ident")
         make_identity(nc, ident[:])
@@ -88,8 +88,9 @@ def tile_list_sage_tm_silu_kernel(tc, xT, c, w4_words, w4_scales, w8_words, w8_s
             bias=silu_zero[:],
         )
 
-        table = [keep.tile([P, T], U32, name="table%d" % h) for h in range(2)]
-        picked = keep.tile([P, 2, G, S], U32, name="picked")
+        table = [keep.tile([P, T], U32, name="table%d" % h, align_bytes=64) for h in range(2)]
+        work = keep.tile([P, 2 * G * S + 3 * P], U32, name="work", align_bytes=64)
+        picked = work[:, 0 : 2 * G * S].rearrange("p (h g j) -> p h g j", h=2, g=G)
 
         def cast_x(n):
             h, t0, t1, nv = X_CHUNKS[n]
@@ -104,17 +105,22 @@ def tile_list_sage_tm_silu_kernel(tc, xT, c, w4_words, w4_scales, w8_words, w8_s
             cols = slice((g * S + j0) // LANES, (g * S + j1) // LANES)
             nc.vector.tensor_copy(picked[:, h, g, j0:j1], table[h][:].indirect(offsets[:, cols]))
 
-        xm = keep.tile([P, S, PACK], BF16, name="xm", align_bytes=64)
-        cb = keep.tile([P, S, PACK], BF16, name="cb", align_bytes=64)
-        xm_codes = keep.tile([P, S], U32, name="xm_codes", align_bytes=64)
+        cb1 = keep.tile([P, HALF, PACK], BF16, name="cb1", align_bytes=64)
+        cb = (work[:, 2 * G * S - P :].bitcast(BF16).rearrange("p (j t) -> p j t", t=PACK), cb1[:])
         xm_scale = keep.tile([P, S], U8, name="xm_scale", align_bytes=64)
         c_codes = keep.tile([P, S], U32, name="c_codes", align_bytes=64)
         c_scale = keep.tile([P, S], U8, name="c_scale", align_bytes=64)
-        pairs = picked[:].bitcast(BF16).rearrange("p h g (j e) -> p g j h e", e=2)
+        pairs = work[:, 0 : 2 * G * S].bitcast(BF16).rearrange("p (h g j e) -> p g j h e", h=2, g=G, e=2)
+
+        def xm_cols(j0, j1):
+            return xm[j0 // HALF][:, j0 % HALF : j0 % HALF + j1 - j0, :]
+
+        def xm_code_cols(j0, j1):
+            return xm_codes[j0 // HALF][:, j0 % HALF : j0 % HALF + j1 - j0]
 
         def maximum(j0, j1):
             nc.vector.tensor_tensor(
-                xm[:, j0:j1, :].rearrange("p j (h e) -> p j h e", e=2),
+                xm_cols(j0, j1).rearrange("p j (h e) -> p j h e", e=2),
                 pairs[:, 0, j0:j1],
                 pairs[:, 1, j0:j1],
                 ALU.max,
@@ -122,16 +128,19 @@ def tile_list_sage_tm_silu_kernel(tc, xT, c, w4_words, w4_scales, w8_words, w8_s
 
         def cast_c(u):
             nc.scalar.copy(
-                cb[:, u * HALF : (u + 1) * HALF, :].rearrange("p (r i) t -> p r t i", i=RUN),
+                cb[u].rearrange("p (r i) t -> p r t i", i=RUN),
                 c_raw[u][:].rearrange("p t (r i) -> p r t i", i=RUN),
             )
 
-        def quantize(codes, scale, src, j0, j1):
-            nc.vector.quantize_mx(
-                out=codes[:, j0:j1].bitcast(FP8X4),
-                scales=scale[:, j0:j1],
-                in_=src[:, j0:j1, :].rearrange("p j t -> p (j t)"),
-            )
+        def quantize(codes, scale, src):
+            nc.vector.quantize_mx(out=codes.bitcast(FP8X4), scales=scale, in_=src.rearrange("p j t -> p (j t)"))
+
+        def quantize_c(u):
+            js = slice(u * HALF, (u + 1) * HALF)
+            quantize(c_codes[:, js], c_scale[:, js], cb[u])
+
+        def quantize_xm(j0, j1):
+            quantize(xm_code_cols(j0, j1), xm_scale[:, j0:j1], xm_cols(j0, j1))
 
         y = [psum.tile([P, M], F32, name="y%d" % jt) for jt in range(S // P)]
 
@@ -151,7 +160,7 @@ def tile_list_sage_tm_silu_kernel(tc, xT, c, w4_words, w4_scales, w8_words, w8_s
             js = slice(jt * P, (jt + 1) * P)
             nc.tensor.matmul_mx(
                 out=y[jt][:, nh * P : (nh + 1) * P],
-                lhsT=xm_codes[:, js].bitcast(FP8X4),
+                lhsT=xm_code_cols(jt * P, (jt + 1) * P).bitcast(FP8X4),
                 lhsT_scale=xm_scale[:, js],
                 rhs=w4[:, 2 * nh * P : 2 * (nh + 1) * P].bitcast(FP4X4),
                 rhs_scale=w_scale[:, nh * P : (nh + 1) * P],
@@ -175,21 +184,29 @@ def tile_list_sage_tm_silu_kernel(tc, xT, c, w4_words, w4_scales, w8_words, w8_s
         cast_x(4)
         cast_c(0)
         cast_c(1)
+        xm0 = keep.tile([P, HALF, PACK], BF16, name="xm0", align_bytes=64)
+        xm1 = keep.tile([P, HALF, PACK], BF16, name="xm1", tag="c_raw1", align_bytes=64)
+        xm = (xm0, xm1)
+        xm_codes1 = keep.tile([P, HALF], U32, name="xm_codes1", align_bytes=64)
+        xm_codes0 = keep.tile([P, HALF], U32, name="xm_codes0", tag="c_raw0", align_bytes=64)
+        xm_codes = (xm_codes0, xm_codes1)
         gather(1, 0, 0, HALF)
         gather(1, 1, 0, HALF)
         gather(1, 0, HALF, S)
         maximum(0, HALF)
+        quantize_c(0)
+        quantize_xm(0, HALF)
         gather(1, 1, HALF, S)
-        quantize(c_codes, c_scale, cb, 0, HALF)
-        quantize(xm_codes, xm_scale, xm, 0, HALF)
-        maximum(HALF, S)
-        quantize(c_codes, c_scale, cb, HALF, S)
-        quantize(xm_codes, xm_scale, xm, HALF, S)
+        quantize_c(1)
+        maximum(2 * P, 3 * P)
+        maximum(3 * P, 4 * P)
+        quantize_xm(2 * P, 3 * P)
+        quantize_xm(3 * P, 4 * P)
         for u in range(2):
             for jt in (2 * u, 2 * u + 1):
                 own_pass(jt)
             for jt in (2 * u, 2 * u + 1):
                 for nh in range(2):
                     neighbour_pass(jt, nh)
-        for jt in range(S // P):
+        for jt in range(4):
             finish(jt)

@@ -23,7 +23,7 @@ RUN = 4
 HALF = S // 2
 LANES = 16
 
-X_CHUNKS = ((0, 0, 1024, 0), (0, 1024, 2048, 704), (1, 0, 896, 0), (1, 896, 1664, 512), (1, 1664, 2048, 256))
+X_CHUNKS = ((0, 0, 1024, 0), (0, 1024, 2048, 704), (1, 0, 1024, 256), (1, 1024, 1536, 512), (1, 1536, 1792, 128), (1, 1792, 2048, 192))
 
 
 def tile_list_sage_tm_silu_kernel(tc, xT, c, w4_words, w4_scales, w8_words, w8_scales, b, offs, out):
@@ -41,7 +41,8 @@ def tile_list_sage_tm_silu_kernel(tc, xT, c, w4_words, w4_scales, w8_words, w8_s
         w4 = keep.tile([P, 2 * M], U8, name="w4", align_bytes=64)
         w8 = keep.tile([P, 4 * M], U8, name="w8", align_bytes=64)
         w_scale = keep.tile([P, 2 * M], U8, name="w_scale", align_bytes=64)
-        b_col = keep.tile([P, 2], F32, name="b_col")
+        b_rows = keep.tile([P, P], F32, name="b_rows")
+        nc.vector.memset(b_rows[:], 0.0)
         nc.vector.memset(w_scale[:].bitcast(U32), 0)
 
         def load_x(n):
@@ -58,11 +59,12 @@ def tile_list_sage_tm_silu_kernel(tc, xT, c, w4_words, w4_scales, w8_words, w8_s
         load_x(0)
         load_x(1)
         nc.sync.dma_start(offsets[:], offs)
-        nc.sync.dma_start(out=b_col[:], in_=b.rearrange("(p e) -> p e", e=2))
+        nc.sync.dma_start(out=b_rows[0:2, :], in_=b.rearrange("(r n) -> r n", r=2))
         load_scales(nc.sync, 1, w8_scales)
         load_x(2)
         load_x(3)
         load_x(4)
+        load_x(5)
         for u in range(2):
             nc.sync.dma_start(out=c_raw[u][:], in_=c_rows[:, :, u * HALF : (u + 1) * HALF])
         nc.sync.dma_start(out=w8[:].bitcast(I32), in_=w8_words[0].rearrange("p n i -> p (n i)").bitcast(I32))
@@ -77,16 +79,15 @@ def tile_list_sage_tm_silu_kernel(tc, xT, c, w4_words, w4_scales, w8_words, w8_s
         nc.vector.memset(zero[:], 0.0)
         nc.scalar.activation(out=silu_zero[:], in_=zero[:], func=ACT.Silu)
 
-        bias_ps = psum.tile([P, 2, P], F32, name="bias_ps")
-        for e in range(2):
-            nc.tensor.transpose(bias_ps[:, e, :], b_col[:, e : e + 1].to_broadcast([P, P]), ident[:])
+        b_col_ps = psum.tile([P, P], F32, name="b_col_ps")
+        nc.tensor.transpose(b_col_ps[:], b_rows[:], ident[:])
+        b_col = keep.tile([P, 2], F32, name="b_col")
+        nc.scalar.activation(out=b_col[:], in_=b_col_ps[:, 0:2], func=ACT.Identity, bias=silu_zero[:])
+        bias_ps = psum.tile([P, M], F32, name="bias_ps")
+        for r in range(2):
+            nc.tensor.transpose(bias_ps[:, r * P : (r + 1) * P], b_col[:, r : r + 1].to_broadcast([P, P]), ident[:])
         bias = keep.tile([P, M], F32, name="bias")
-        nc.scalar.activation(
-            out=bias[:].rearrange("p (n e) -> p n e", e=2),
-            in_=bias_ps[:].rearrange("p e n -> p n e"),
-            func=ACT.Identity,
-            bias=silu_zero[:],
-        )
+        nc.scalar.copy(bias[:], bias_ps[:])
 
         table = [keep.tile([P, T], U32, name="table%d" % h, align_bytes=64) for h in range(2)]
         work = keep.tile([P, 2 * G * S + 3 * P], U32, name="work", align_bytes=64)
@@ -173,7 +174,8 @@ def tile_list_sage_tm_silu_kernel(tc, xT, c, w4_words, w4_scales, w8_words, w8_s
             res = keep.tile([P, M], F32, name="res%d" % jt)
             nc.vector.tensor_tensor(pre[:], y[jt][:], bias[:], ALU.add)
             nc.scalar.activation(out=res[:], in_=pre[:], func=ACT.Silu)
-            nc.sync.dma_start(out=out[jt * P : (jt + 1) * P, :], in_=res[:])
+            queue = nc.scalar if jt == S // P - 1 else nc.sync
+            queue.dma_start(out=out[jt * P : (jt + 1) * P, :], in_=res[:])
 
         cast_x(0)
         cast_x(1)
@@ -182,6 +184,7 @@ def tile_list_sage_tm_silu_kernel(tc, xT, c, w4_words, w4_scales, w8_words, w8_s
         cast_x(2)
         cast_x(3)
         cast_x(4)
+        cast_x(5)
         cast_c(0)
         cast_c(1)
         xm0 = keep.tile([P, HALF, PACK], BF16, name="xm0", align_bytes=64)

@@ -23,7 +23,7 @@ RUN = 4
 HALF = S // 2
 LANES = 16
 
-X_CHUNKS = ((0, 0, 1024, 0), (0, 1024, 2048, 704), (1, 0, 1024, 256), (1, 1024, 1536, 512), (1, 1536, 1792, 128), (1, 1792, 2048, 192))
+X_CHUNKS = ((0, 0, 1280, 832), (0, 1280, 2048, 512), (1, 0, 1024, 320), (1, 1024, 1792, 512), (1, 1792, 2048, 160))
 
 
 def tile_list_sage_tm_silu_kernel(tc, xT, c, w4_words, w4_scales, w8_words, w8_scales, b, offs, out):
@@ -60,13 +60,12 @@ def tile_list_sage_tm_silu_kernel(tc, xT, c, w4_words, w4_scales, w8_words, w8_s
         load_x(1)
         nc.sync.dma_start(offsets[:], offs)
         nc.sync.dma_start(out=b_rows[0:2, :], in_=b.rearrange("(r n) -> r n", r=2))
-        load_scales(nc.sync, 1, w8_scales)
         load_x(2)
         load_x(3)
         load_x(4)
-        load_x(5)
-        for u in range(2):
-            nc.sync.dma_start(out=c_raw[u][:], in_=c_rows[:, :, u * HALF : (u + 1) * HALF])
+        nc.sync.dma_start(out=c_raw[0][:], in_=c_rows[:, :, 0:HALF])
+        load_scales(nc.sync, 1, w8_scales)
+        nc.sync.dma_start(out=c_raw[1][:], in_=c_rows[:, :, HALF:S])
         nc.sync.dma_start(out=w8[:].bitcast(I32), in_=w8_words[0].rearrange("p n i -> p (n i)").bitcast(I32))
         nc.sync.dma_start(out=w4[:].bitcast(I32), in_=w4_words[0].bitcast(I32))
         load_scales(nc.sync, 0, w4_scales)
@@ -184,7 +183,6 @@ def tile_list_sage_tm_silu_kernel(tc, xT, c, w4_words, w4_scales, w8_words, w8_s
         cast_x(2)
         cast_x(3)
         cast_x(4)
-        cast_x(5)
         cast_c(0)
         cast_c(1)
         xm0 = keep.tile([P, HALF, PACK], BF16, name="xm0", align_bytes=64)

@@ -23,7 +23,7 @@ RUN = 4
 HALF = S // 2
 LANES = 16
 
-X_CHUNKS = ((0, 0, 1280, 832), (0, 1280, 2048, 512), (1, 0, 1024, 320), (1, 1024, 1792, 512), (1, 1792, 2048, 160))
+X_CHUNKS = ((0, 0, 1024, 512), (0, 1024, 1792, 512), (0, 1792, 2048, 192), (1, 0, 1024, 320), (1, 1024, 1792, 544), (1, 1792, 2048, 192))
 
 
 def tile_list_sage_tm_silu_kernel(tc, xT, c, w4_words, w4_scales, w8_words, w8_scales, b, offs, out):
@@ -49,26 +49,29 @@ def tile_list_sage_tm_silu_kernel(tc, xT, c, w4_words, w4_scales, w8_words, w8_s
             h, t0, t1, nv = X_CHUNKS[n]
             nc.sync.dma_start(out=x_raw[n][:], in_=x_rows[:, 2 * h : 2 * h + 2, t0:t1])
 
-        def load_scales(queue, w, src):
-            for q in range(4):
-                queue.dma_start(
+        def load_scales(w, quadrants):
+            for q in quadrants:
+                nc.sync.dma_start(
                     out=w_scale[32 * q : 32 * q + 4, w * M : (w + 1) * M].bitcast(I32),
-                    in_=src[0, 4 * q : 4 * q + 4, :].bitcast(I32),
+                    in_=(w4_scales, w8_scales)[w][0, 4 * q : 4 * q + 4, :].bitcast(I32),
                 )
 
         load_x(0)
-        load_x(1)
-        nc.sync.dma_start(offsets[:], offs)
         nc.sync.dma_start(out=b_rows[0:2, :], in_=b.rearrange("(r n) -> r n", r=2))
+        load_x(1)
         load_x(2)
+        nc.sync.dma_start(offsets[:], offs)
+        load_scales(1, (0, 1))
         load_x(3)
+        load_scales(1, (2, 3))
+        load_scales(0, (0, 1))
         load_x(4)
+        load_x(5)
+        load_scales(0, (2, 3))
         nc.sync.dma_start(out=c_raw[0][:], in_=c_rows[:, :, 0:HALF])
-        load_scales(nc.sync, 1, w8_scales)
         nc.sync.dma_start(out=c_raw[1][:], in_=c_rows[:, :, HALF:S])
         nc.sync.dma_start(out=w8[:].bitcast(I32), in_=w8_words[0].rearrange("p n i -> p (n i)").bitcast(I32))
         nc.sync.dma_start(out=w4[:].bitcast(I32), in_=w4_words[0].bitcast(I32))
-        load_scales(nc.sync, 0, w4_scales)
 
         ident = keep.tile([P, P], F32, name="ident")
         make_identity(nc, ident[:])
@@ -178,11 +181,12 @@ def tile_list_sage_tm_silu_kernel(tc, xT, c, w4_words, w4_scales, w8_words, w8_s
 
         cast_x(0)
         cast_x(1)
+        cast_x(2)
         gather(0, 0, 0, S)
         gather(0, 1, 0, S)
-        cast_x(2)
         cast_x(3)
         cast_x(4)
+        cast_x(5)
         cast_c(0)
         cast_c(1)
         xm0 = keep.tile([P, HALF, PACK], BF16, name="xm0", align_bytes=64)

@@ -76,15 +76,10 @@ def tile_list_sage_tm_silu_kernel(tc, xT, c, w4_words, w4_scales, w8_words, w8_s
         ident = keep.tile([P, P], F32, name="ident")
         make_identity(nc, ident[:])
 
-        zero = keep.tile([P, 1], F32, name="zero")
-        silu_zero = keep.tile([P, 1], F32, name="silu_zero")
-        nc.vector.memset(zero[:], 0.0)
-        nc.scalar.activation(out=silu_zero[:], in_=zero[:], func=ACT.Silu)
-
         b_col_ps = psum.tile([P, P], F32, name="b_col_ps")
         nc.tensor.transpose(b_col_ps[:], b_rows[:], ident[:])
         b_col = keep.tile([P, 2], F32, name="b_col")
-        nc.scalar.activation(out=b_col[:], in_=b_col_ps[:, 0:2], func=ACT.Identity, bias=silu_zero[:])
+        nc.scalar.copy(b_col[:], b_col_ps[:, 0:2])
         bias_ps = psum.tile([P, M], F32, name="bias_ps")
         for r in range(2):
             nc.tensor.transpose(bias_ps[:, r * P : (r + 1) * P], b_col[:, r : r + 1].to_broadcast([P, P]), ident[:])

@@ -23,7 +23,7 @@ RUN = 4
 HALF = S // 2
 LANES = 16
 
-X_CHUNKS = ((0, 0, 1024, 512), (0, 1024, 1792, 512), (0, 1792, 2048, 192), (1, 0, 1024, 320), (1, 1024, 1792, 544), (1, 1792, 2048, 192))
+X_CHUNKS = ((0, 0, 1024, 704), (0, 1024, 1792, 512), (0, 1792, 2048, 192), (1, 0, 1024, 320), (1, 1024, 1792, 544), (1, 1792, 2048, 192))
 
 
 def tile_list_sage_tm_silu_kernel(tc, xT, c, w4_words, w4_scales, w8_words, w8_scales, b, offs, out):
@@ -36,7 +36,12 @@ def tile_list_sage_tm_silu_kernel(tc, xT, c, w4_words, w4_scales, w8_words, w8_s
         x_rows = xT.rearrange("(p i) t -> p i t", i=PACK)
         c_rows = c.rearrange("(p i) j -> p i j", i=PACK)
 
-        x_raw = [keep.tile([P, 2, t1 - t0], F32, name="x_raw%d" % n) for n, (h, t0, t1, nv) in enumerate(X_CHUNKS)]
+        x_flat = xT.rearrange("(p i) t -> p (i t)", i=PACK)
+        x_first = keep.tile([P, 2 * T], F32, name="x_first")
+        x_raw = [
+            x_first[:].rearrange("p (e t) -> p e t", e=2)[:, :, t0:t1] if h == 0 else keep.tile([P, 2, t1 - t0], F32, name="x_raw%d" % n)[:]
+            for n, (h, t0, t1, nv) in enumerate(X_CHUNKS)
+        ]
         c_raw = [keep.tile([P, PACK, HALF], F32, name="c_raw%d" % u, align_bytes=64) for u in range(2)]
         w4 = keep.tile([P, 2 * M], U8, name="w4", align_bytes=64)
         w8 = keep.tile([P, 4 * M], U8, name="w8", align_bytes=64)
@@ -47,7 +52,11 @@ def tile_list_sage_tm_silu_kernel(tc, xT, c, w4_words, w4_scales, w8_words, w8_s
 
         def load_x(n):
             h, t0, t1, nv = X_CHUNKS[n]
-            nc.sync.dma_start(out=x_raw[n][:], in_=x_rows[:, 2 * h : 2 * h + 2, t0:t1])
+            if h == 0:
+                run = slice(T + t0 if t0 else 0, T + t1)
+                nc.sync.dma_start(out=x_first[:, run], in_=x_flat[:, run])
+            else:
+                nc.sync.dma_start(out=x_raw[n], in_=x_rows[:, 2 * h : 2 * h + 2, t0:t1])
 
         def load_scales(w, quadrants):
             for q in quadrants:
@@ -140,39 +149,47 @@ def tile_list_sage_tm_silu_kernel(tc, xT, c, w4_words, w4_scales, w8_words, w8_s
         def quantize_xm(j0, j1):
             quantize(xm_code_cols(j0, j1), xm_scale[:, j0:j1], xm_cols(j0, j1))
 
-        y = [psum.tile([P, M], F32, name="y%d" % jt) for jt in range(S // P)]
+        pieces = [(0, 0, M), (1, 0, M), (2, 0, M), (3, 0, P), (3, P, M)]
+        y = [psum.tile([P, n1 - n0], F32, name="y%d" % k) for k, (jt, n0, n1) in enumerate(pieces)]
+        pre_late = [keep.tile([P, M], F32, name="pre%d" % jt) for jt in (2, 3)]
+        pre = [work[:, g * S + HALF : (g + 1) * S].bitcast(F32) for g in range(G)] + [t[:] for t in pre_late]
+        res = [keep.tile([P, M], F32, name="res%d" % jt) for jt in range(S // P)]
 
-        def own_pass(jt):
+        def own_pass(k):
+            jt, n0, n1 = pieces[k]
             js = slice(jt * P, (jt + 1) * P)
             nc.tensor.matmul_mx(
-                out=y[jt][:],
+                out=y[k][:],
                 lhsT=c_codes[:, js].bitcast(FP8X4),
                 lhsT_scale=c_scale[:, js],
-                rhs=w8[:].bitcast(FP8X4),
-                rhs_scale=w_scale[:, M : 2 * M],
+                rhs=w8[:, 4 * n0 : 4 * n1].bitcast(FP8X4),
+                rhs_scale=w_scale[:, M + n0 : M + n1],
                 start=True,
                 stop=False,
             )
 
-        def neighbour_pass(jt, nh):
-            js = slice(jt * P, (jt + 1) * P)
+        def neighbour_pass(k):
+            jt, n0, n1 = pieces[k]
             nc.tensor.matmul_mx(
-                out=y[jt][:, nh * P : (nh + 1) * P],
+                out=y[k][:],
                 lhsT=xm_code_cols(jt * P, (jt + 1) * P).bitcast(FP8X4),
-                lhsT_scale=xm_scale[:, js],
-                rhs=w4[:, 2 * nh * P : 2 * (nh + 1) * P].bitcast(FP4X4),
-                rhs_scale=w_scale[:, nh * P : (nh + 1) * P],
+                lhsT_scale=xm_scale[:, jt * P : (jt + 1) * P],
+                rhs=w4[:, 2 * n0 : 2 * n1].bitcast(FP4X4),
+                rhs_scale=w_scale[:, n0:n1],
                 start=False,
-                stop=(nh == 1),
+                stop=True,
             )
 
-        def finish(jt):
-            pre = keep.tile([P, M], F32, name="pre%d" % jt)
-            res = keep.tile([P, M], F32, name="res%d" % jt)
-            nc.vector.tensor_tensor(pre[:], y[jt][:], bias[:], ALU.add)
-            nc.scalar.activation(out=res[:], in_=pre[:], func=ACT.Silu)
-            queue = nc.scalar if jt == S // P - 1 else nc.sync
-            queue.dma_start(out=out[jt * P : (jt + 1) * P, :], in_=res[:])
+        def finish(k):
+            jt, n0, n1 = pieces[k]
+            width = P if k == 0 else n1 - n0
+            for m0 in range(n0, n1, width):
+                ms = slice(m0, m0 + width)
+                nc.vector.tensor_tensor(pre[jt][:, ms], y[k][:, m0 - n0 : m0 - n0 + width], bias[:, ms], ALU.add)
+                nc.scalar.activation(out=res[jt][:, ms], in_=pre[jt][:, ms], func=ACT.Silu)
+            if n1 == M:
+                queue = nc.scalar if jt == S // P - 1 else nc.sync
+                queue.dma_start(out=out[jt * P : (jt + 1) * P, :], in_=res[jt][:])
 
         cast_x(0)
         cast_x(1)
@@ -202,11 +219,10 @@ def tile_list_sage_tm_silu_kernel(tc, xT, c, w4_words, w4_scales, w8_words, w8_s
         maximum(3 * P, 4 * P)
         quantize_xm(2 * P, 3 * P)
         quantize_xm(3 * P, 4 * P)
-        for u in range(2):
-            for jt in (2 * u, 2 * u + 1):
-                own_pass(jt)
-            for jt in (2 * u, 2 * u + 1):
-                for nh in range(2):
-                    neighbour_pass(jt, nh)
-        for jt in range(4):
-            finish(jt)
+        for ks in ((0, 1), (2, 3, 4)):
+            for k in ks:
+                own_pass(k)
+            for k in ks:
+                neighbour_pass(k)
+        for k in range(len(pieces)):
+            finish(k)

@@ -23,7 +23,16 @@ RUN = 4
 HALF = S // 2
 LANES = 16
 
-X_CHUNKS = ((0, 0, 1024, 704), (0, 1024, 1792, 512), (0, 1792, 2048, 192), (1, 0, 1024, 320), (1, 1024, 1792, 544), (1, 1792, 2048, 192))
+X_CHUNKS = (
+    (0, 0, 1408, 896),
+    (0, 1408, 2048, 448),
+    (1, 0, 1024, 320),
+    (1, 1024, 1664, 448),
+    (1, 1664, 1920, 192),
+    (1, 1920, 2048, 128),
+)
+
+SUMS = ((0, 0, M), (1, 0, M), (2, 0, M), (3, 0, P), (3, P, M))
 
 
 def tile_list_sage_tm_silu_kernel(tc, xT, c, w4_words, w4_scales, w8_words, w8_scales, b, offs, out):
@@ -36,12 +45,7 @@ def tile_list_sage_tm_silu_kernel(tc, xT, c, w4_words, w4_scales, w8_words, w8_s
         x_rows = xT.rearrange("(p i) t -> p i t", i=PACK)
         c_rows = c.rearrange("(p i) j -> p i j", i=PACK)
 
-        x_flat = xT.rearrange("(p i) t -> p (i t)", i=PACK)
-        x_first = keep.tile([P, 2 * T], F32, name="x_first")
-        x_raw = [
-            x_first[:].rearrange("p (e t) -> p e t", e=2)[:, :, t0:t1] if h == 0 else keep.tile([P, 2, t1 - t0], F32, name="x_raw%d" % n)[:]
-            for n, (h, t0, t1, nv) in enumerate(X_CHUNKS)
-        ]
+        x_raw = [keep.tile([P, 2, t1 - t0], F32, name="x_raw%d" % n) for n, (h, t0, t1, nv) in enumerate(X_CHUNKS)]
         c_raw = [keep.tile([P, PACK, HALF], F32, name="c_raw%d" % u, align_bytes=64) for u in range(2)]
         w4 = keep.tile([P, 2 * M], U8, name="w4", align_bytes=64)
         w8 = keep.tile([P, 4 * M], U8, name="w8", align_bytes=64)
@@ -52,11 +56,7 @@ def tile_list_sage_tm_silu_kernel(tc, xT, c, w4_words, w4_scales, w8_words, w8_s
 
         def load_x(n):
             h, t0, t1, nv = X_CHUNKS[n]
-            if h == 0:
-                run = slice(T + t0 if t0 else 0, T + t1)
-                nc.sync.dma_start(out=x_first[:, run], in_=x_flat[:, run])
-            else:
-                nc.sync.dma_start(out=x_raw[n], in_=x_rows[:, 2 * h : 2 * h + 2, t0:t1])
+            nc.sync.dma_start(out=x_raw[n][:], in_=x_rows[:, 2 * h : 2 * h + 2, t0:t1])
 
         def load_scales(w, quadrants):
             for q in quadrants:
@@ -68,16 +68,16 @@ def tile_list_sage_tm_silu_kernel(tc, xT, c, w4_words, w4_scales, w8_words, w8_s
         load_x(0)
         nc.sync.dma_start(out=b_rows[0:2, :], in_=b.rearrange("(r n) -> r n", r=2))
         load_x(1)
-        load_x(2)
         nc.sync.dma_start(offsets[:], offs)
         load_scales(1, (0, 1))
-        load_x(3)
+        load_x(2)
         load_scales(1, (2, 3))
         load_scales(0, (0, 1))
+        load_x(3)
         load_x(4)
         load_x(5)
-        load_scales(0, (2, 3))
         nc.sync.dma_start(out=c_raw[0][:], in_=c_rows[:, :, 0:HALF])
+        load_scales(0, (2, 3))
         nc.sync.dma_start(out=c_raw[1][:], in_=c_rows[:, :, HALF:S])
         nc.sync.dma_start(out=w8[:].bitcast(I32), in_=w8_words[0].rearrange("p n i -> p (n i)").bitcast(I32))
         nc.sync.dma_start(out=w4[:].bitcast(I32), in_=w4_words[0].bitcast(I32))
@@ -149,17 +149,16 @@ def tile_list_sage_tm_silu_kernel(tc, xT, c, w4_words, w4_scales, w8_words, w8_s
         def quantize_xm(j0, j1):
             quantize(xm_code_cols(j0, j1), xm_scale[:, j0:j1], xm_cols(j0, j1))
 
-        pieces = [(0, 0, M), (1, 0, M), (2, 0, M), (3, 0, P), (3, P, M)]
-        y = [psum.tile([P, n1 - n0], F32, name="y%d" % k) for k, (jt, n0, n1) in enumerate(pieces)]
+        y = [psum.tile([P, n1 - n0], F32, name="y%d" % s) for s, (jt, n0, n1) in enumerate(SUMS)]
         pre_late = [keep.tile([P, M], F32, name="pre%d" % jt) for jt in (2, 3)]
         pre = [work[:, g * S + HALF : (g + 1) * S].bitcast(F32) for g in range(G)] + [t[:] for t in pre_late]
         res = [keep.tile([P, M], F32, name="res%d" % jt) for jt in range(S // P)]
 
-        def own_pass(k):
-            jt, n0, n1 = pieces[k]
+        def own_pass(s):
+            jt, n0, n1 = SUMS[s]
             js = slice(jt * P, (jt + 1) * P)
             nc.tensor.matmul_mx(
-                out=y[k][:],
+                out=y[s][:],
                 lhsT=c_codes[:, js].bitcast(FP8X4),
                 lhsT_scale=c_scale[:, js],
                 rhs=w8[:, 4 * n0 : 4 * n1].bitcast(FP8X4),
@@ -168,10 +167,10 @@ def tile_list_sage_tm_silu_kernel(tc, xT, c, w4_words, w4_scales, w8_words, w8_s
                 stop=False,
             )
 
-        def neighbour_pass(k):
-            jt, n0, n1 = pieces[k]
+        def neighbour_pass(s):
+            jt, n0, n1 = SUMS[s]
             nc.tensor.matmul_mx(
-                out=y[k][:],
+                out=y[s][:],
                 lhsT=xm_code_cols(jt * P, (jt + 1) * P).bitcast(FP8X4),
                 lhsT_scale=xm_scale[:, jt * P : (jt + 1) * P],
                 rhs=w4[:, 2 * n0 : 2 * n1].bitcast(FP4X4),
@@ -180,12 +179,11 @@ def tile_list_sage_tm_silu_kernel(tc, xT, c, w4_words, w4_scales, w8_words, w8_s
                 stop=True,
             )
 
-        def finish(k):
-            jt, n0, n1 = pieces[k]
-            width = P if k == 0 else n1 - n0
-            for m0 in range(n0, n1, width):
-                ms = slice(m0, m0 + width)
-                nc.vector.tensor_tensor(pre[jt][:, ms], y[k][:, m0 - n0 : m0 - n0 + width], bias[:, ms], ALU.add)
+        def finish(s):
+            jt, n0, n1 = SUMS[s]
+            for m0 in range(n0, n1, P):
+                ms = slice(m0, m0 + P)
+                nc.vector.tensor_tensor(pre[jt][:, ms], y[s][:, m0 - n0 : m0 - n0 + P], bias[:, ms], ALU.add)
                 nc.scalar.activation(out=res[jt][:, ms], in_=pre[jt][:, ms], func=ACT.Silu)
             if n1 == M:
                 queue = nc.scalar if jt == S // P - 1 else nc.sync
@@ -193,9 +191,9 @@ def tile_list_sage_tm_silu_kernel(tc, xT, c, w4_words, w4_scales, w8_words, w8_s
 
         cast_x(0)
         cast_x(1)
-        cast_x(2)
         gather(0, 0, 0, S)
         gather(0, 1, 0, S)
+        cast_x(2)
         cast_x(3)
         cast_x(4)
         cast_x(5)
@@ -219,10 +217,10 @@ def tile_list_sage_tm_silu_kernel(tc, xT, c, w4_words, w4_scales, w8_words, w8_s
         maximum(3 * P, 4 * P)
         quantize_xm(2 * P, 3 * P)
         quantize_xm(3 * P, 4 * P)
-        for ks in ((0, 1), (2, 3, 4)):
-            for k in ks:
-                own_pass(k)
-            for k in ks:
-                neighbour_pass(k)
-        for k in range(len(pieces)):
-            finish(k)
+        for group in ((0, 1), (2, 3, 4)):
+            for s in group:
+                own_pass(s)
+            for s in group:
+                neighbour_pass(s)
+        for s in range(len(SUMS)):
+            finish(s)

@@ -22,6 +22,7 @@ PACK = 4
 RUN = 4
 HALF = S // 2
 LANES = 16
+C_ON_GPSIMD = 96
 
 X_CHUNKS = (
     (0, 0, 1408, 896),
@@ -134,10 +135,20 @@ def tile_list_sage_tm_silu_kernel(tc, xT, c, w4_words, w4_scales, w8_words, w8_s
             )
 
         def cast_c(u):
+            shared = C_ON_GPSIMD if u == 0 else 0
             nc.scalar.copy(
-                cb[u].rearrange("p (r i) t -> p r t i", i=RUN),
-                c_raw[u][:].rearrange("p t (r i) -> p r t i", i=RUN),
+                cb[u][:, shared:, :].rearrange("p (r i) t -> p r t i", i=RUN),
+                c_raw[u][:, :, shared:].rearrange("p t (r i) -> p r t i", i=RUN),
             )
+            if shared:
+                nc.gpsimd.tensor_scalar(
+                    cb[u][:, 0:shared, :].rearrange("p (r i) t -> p r t i", i=RUN),
+                    c_raw[u][:, :, 0:shared].rearrange("p t (r i) -> p r t i", i=RUN),
+                    1.0,
+                    0.0,
+                    ALU.mult,
+                    ALU.add,
+                )
 
         def quantize(codes, scale, src):
             nc.vector.quantize_mx(out=codes.bitcast(FP8X4), scales=scale, in_=src.rearrange("p j t -> p (j t)"))

from contextlib import ExitStack

import concourse.mybir as mybir
from concourse.masks import make_identity

G, K, M, T, S = 2, 512, 256, 2048, 512
FLOPS = 2 * 2 * K * M * S

F32 = mybir.dt.float32
BF16 = mybir.dt.bfloat16
U32 = mybir.dt.uint32
I32 = mybir.dt.int32
U16 = mybir.dt.uint16
U8 = mybir.dt.uint8
FP8X4 = mybir.dt.float8_e4m3fn_x4
FP4X4 = mybir.dt.float4_e2m1fn_x4
ACT = mybir.ActivationFunctionType
ALU = mybir.AluOpType

P = 128
PACK = 4
RUN = 4
HALF = S // 2
LANES = 16
C_ON_GPSIMD = 96

X_CHUNKS = (
    (0, 0, 1408, 896),
    (0, 1408, 2048, 448),
    (1, 0, 1024, 320),
    (1, 1024, 1664, 448),
    (1, 1664, 1920, 192),
    (1, 1920, 2048, 128),
)

SUMS = ((0, 0, M), (1, 0, M), (2, 0, M), (3, 0, P), (3, P, M))


def tile_list_sage_tm_silu_kernel(tc, xT, c, w4_words, w4_scales, w8_words, w8_scales, b, offs, out):
    nc = tc.nc
    with ExitStack() as ctx:
        keep = ctx.enter_context(tc.tile_pool(name="keep", bufs=1))
        psum = ctx.enter_context(tc.psum_pool(name="psum", bufs=1))

        offsets = keep.tile([P, G * S // LANES], U16, name="offsets")
        x_rows = xT.rearrange("(p i) t -> p i t", i=PACK)
        c_rows = c.rearrange("(p i) j -> p i j", i=PACK)

        x_raw = [keep.tile([P, 2, t1 - t0], F32, name="x_raw%d" % n) for n, (h, t0, t1, nv) in enumerate(X_CHUNKS)]
        c_raw = [keep.tile([P, PACK, HALF], F32, name="c_raw%d" % u, align_bytes=64) for u in range(2)]
        w4 = keep.tile([P, 2 * M], U8, name="w4", align_bytes=64)
        w8 = keep.tile([P, 4 * M], U8, name="w8", align_bytes=64)
        w_scale = keep.tile([P, 2 * M], U8, name="w_scale", align_bytes=64)
        b_rows = keep.tile([P, P], F32, name="b_rows")
        nc.vector.memset(b_rows[:], 0.0)
        nc.vector.memset(w_scale[:].bitcast(U32), 0)

        def load_x(n):
            h, t0, t1, nv = X_CHUNKS[n]
            nc.sync.dma_start(out=x_raw[n][:], in_=x_rows[:, 2 * h : 2 * h + 2, t0:t1])

        def load_scales(w, quadrants):
            for q in quadrants:
                nc.sync.dma_start(
                    out=w_scale[32 * q : 32 * q + 4, w * M : (w + 1) * M].bitcast(I32),
                    in_=(w4_scales, w8_scales)[w][0, 4 * q : 4 * q + 4, :].bitcast(I32),
                )

        load_x(0)
        nc.sync.dma_start(out=b_rows[0:2, :], in_=b.rearrange("(r n) -> r n", r=2))
        load_x(1)
        nc.sync.dma_start(offsets[:], offs)
        load_scales(1, (0, 1))
        load_x(2)
        load_scales(1, (2, 3))
        load_scales(0, (0, 1))
        load_x(3)
        load_x(4)
        load_x(5)
        nc.sync.dma_start(out=c_raw[0][:], in_=c_rows[:, :, 0:HALF])
        load_scales(0, (2, 3))
        nc.sync.dma_start(out=c_raw[1][:], in_=c_rows[:, :, HALF:S])
        nc.sync.dma_start(out=w8[:].bitcast(I32), in_=w8_words[0].rearrange("p n i -> p (n i)").bitcast(I32))
        nc.sync.dma_start(out=w4[:].bitcast(I32), in_=w4_words[0].bitcast(I32))

        ident = keep.tile([P, P], F32, name="ident")
        make_identity(nc, ident[:])

        b_col_ps = psum.tile([P, P], F32, name="b_col_ps")
        nc.tensor.transpose(b_col_ps[:], b_rows[:], ident[:])
        b_col = keep.tile([P, 2], F32, name="b_col")
        nc.scalar.copy(b_col[:], b_col_ps[:, 0:2])
        bias_ps = psum.tile([P, M], F32, name="bias_ps")
        for r in range(2):
            nc.tensor.transpose(bias_ps[:, r * P : (r + 1) * P], b_col[:, r : r + 1].to_broadcast([P, P]), ident[:])
        bias = keep.tile([P, M], F32, name="bias")
        nc.scalar.copy(bias[:], bias_ps[:])

        table = [keep.tile([P, T], U32, name="table%d" % h, align_bytes=64) for h in range(2)]
        work = keep.tile([P, 2 * G * S + 3 * P], U32, name="work", align_bytes=64)
        picked = work[:, 0 : 2 * G * S].rearrange("p (h g j) -> p h g j", h=2, g=G)

        def cast_x(n):
            h, t0, t1, nv = X_CHUNKS[n]
            for a, z, copy in ((0, nv, nc.vector.tensor_copy), (nv, t1 - t0, nc.scalar.copy)):
                if z > a:
                    copy(
                        table[h][:].bitcast(BF16)[:, 2 * (t0 + a) : 2 * (t0 + z)].rearrange("p (r i e) -> p r e i", i=RUN, e=2),
                        x_raw[n][:, :, a:z].rearrange("p e (r i) -> p r e i", i=RUN),
                    )

        def gather(h, g, j0, j1):
            cols = slice((g * S + j0) // LANES, (g * S + j1) // LANES)
            nc.vector.tensor_copy(picked[:, h, g, j0:j1], table[h][:].indirect(offsets[:, cols]))

        cb1 = keep.tile([P, HALF, PACK], BF16, name="cb1", align_bytes=64)
        cb = (work[:, 2 * G * S - P :].bitcast(BF16).rearrange("p (j t) -> p j t", t=PACK), cb1[:])
        xm_scale = keep.tile([P, S], U8, name="xm_scale", align_bytes=64)
        c_codes = keep.tile([P, S], U32, name="c_codes", align_bytes=64)
        c_scale = keep.tile([P, S], U8, name="c_scale", align_bytes=64)
        pairs = work[:, 0 : 2 * G * S].bitcast(BF16).rearrange("p (h g j e) -> p g j h e", h=2, g=G, e=2)

        def xm_cols(j0, j1):
            return xm[j0 // HALF][:, j0 % HALF : j0 % HALF + j1 - j0, :]

        def xm_code_cols(j0, j1):
            return xm_codes[j0 // HALF][:, j0 % HALF : j0 % HALF + j1 - j0]

        def maximum(j0, j1):
            nc.vector.tensor_tensor(
                xm_cols(j0, j1).rearrange("p j (h e) -> p j h e", e=2),
                pairs[:, 0, j0:j1],
                pairs[:, 1, j0:j1],
                ALU.max,
            )

        def cast_c(u):
            shared = C_ON_GPSIMD if u == 0 else 0
            nc.scalar.copy(
                cb[u][:, shared:, :].rearrange("p (r i) t -> p r t i", i=RUN),
                c_raw[u][:, :, shared:].rearrange("p t (r i) -> p r t i", i=RUN),
            )
            if shared:
                nc.gpsimd.tensor_scalar(
                    cb[u][:, 0:shared, :].rearrange("p (r i) t -> p r t i", i=RUN),
                    c_raw[u][:, :, 0:shared].rearrange("p t (r i) -> p r t i", i=RUN),
                    1.0,
                    0.0,
                    ALU.mult,
                    ALU.add,
                )

        def quantize(codes, scale, src):
            nc.vector.quantize_mx(out=codes.bitcast(FP8X4), scales=scale, in_=src.rearrange("p j t -> p (j t)"))

        def quantize_c(u):
            js = slice(u * HALF, (u + 1) * HALF)
            quantize(c_codes[:, js], c_scale[:, js], cb[u])

        def quantize_xm(j0, j1):
            quantize(xm_code_cols(j0, j1), xm_scale[:, j0:j1], xm_cols(j0, j1))

        y = [psum.tile([P, n1 - n0], F32, name="y%d" % s) for s, (jt, n0, n1) in enumerate(SUMS)]
        pre_late = [keep.tile([P, M], F32, name="pre%d" % jt) for jt in (2, 3)]
        pre = [work[:, g * S + HALF : (g + 1) * S].bitcast(F32) for g in range(G)] + [t[:] for t in pre_late]
        res = [keep.tile([P, M], F32, name="res%d" % jt) for jt in range(S // P)]

        def own_pass(s):
            jt, n0, n1 = SUMS[s]
            js = slice(jt * P, (jt + 1) * P)
            nc.tensor.matmul_mx(
                out=y[s][:],
                lhsT=c_codes[:, js].bitcast(FP8X4),
                lhsT_scale=c_scale[:, js],
                rhs=w8[:, 4 * n0 : 4 * n1].bitcast(FP8X4),
                rhs_scale=w_scale[:, M + n0 : M + n1],
                start=True,
                stop=False,
            )

        def neighbour_pass(s):
            jt, n0, n1 = SUMS[s]
            nc.tensor.matmul_mx(
                out=y[s][:],
                lhsT=xm_code_cols(jt * P, (jt + 1) * P).bitcast(FP8X4),
                lhsT_scale=xm_scale[:, jt * P : (jt + 1) * P],
                rhs=w4[:, 2 * n0 : 2 * n1].bitcast(FP4X4),
                rhs_scale=w_scale[:, n0:n1],
                start=False,
                stop=True,
            )

        def finish(s):
            jt, n0, n1 = SUMS[s]
            for m0 in range(n0, n1, P):
                ms = slice(m0, m0 + P)
                nc.vector.tensor_tensor(pre[jt][:, ms], y[s][:, m0 - n0 : m0 - n0 + P], bias[:, ms], ALU.add)
                nc.scalar.activation(out=res[jt][:, ms], in_=pre[jt][:, ms], func=ACT.Silu)
            if n1 == M:
                queue = nc.scalar if jt == S // P - 1 else nc.sync
                queue.dma_start(out=out[jt * P : (jt + 1) * P, :], in_=res[jt][:])

        cast_x(0)
        cast_x(1)
        gather(0, 0, 0, S)
        gather(0, 1, 0, S)
        cast_x(2)
        cast_x(3)
        cast_x(4)
        cast_x(5)
        cast_c(0)
        cast_c(1)
        xm0 = keep.tile([P, HALF, PACK], BF16, name="xm0", align_bytes=64)
        xm1 = keep.tile([P, HALF, PACK], BF16, name="xm1", tag="c_raw1", align_bytes=64)
        xm = (xm0, xm1)
        xm_codes1 = keep.tile([P, HALF], U32, name="xm_codes1", align_bytes=64)
        xm_codes0 = keep.tile([P, HALF], U32, name="xm_codes0", tag="c_raw0", align_bytes=64)
        xm_codes = (xm_codes0, xm_codes1)
        gather(1, 0, 0, HALF)
        gather(1, 1, 0, HALF)
        gather(1, 0, HALF, S)
        maximum(0, HALF)
        quantize_c(0)
        quantize_xm(0, HALF)
        gather(1, 1, HALF, S)
        quantize_c(1)
        maximum(2 * P, 3 * P)
        maximum(3 * P, 4 * P)
        quantize_xm(2 * P, 3 * P)
        quantize_xm(3 * P, 4 * P)
        for group in ((0, 1), (2, 3, 4)):
            for s in group:
                own_pass(s)
            for s in group:
                neighbour_pass(s)
        for s in range(len(SUMS)):
            finish(s)
